import numpy as np
import ml_dtypes


def mxq(x, axis, fmt="e4m3"):
    dtype, down = {"e4m3": (ml_dtypes.float8_e4m3fn, 7), "e5m2": (ml_dtypes.float8_e5m2, 14)}[fmt]
    v = np.moveaxis(np.asarray(x, np.float32).astype(ml_dtypes.bfloat16).astype(np.float64), axis, -1)
    blocks = v.reshape(v.shape[:-1] + (-1, 32))
    amax = np.abs(blocks).max(-1, keepdims=True)
    byte = np.maximum(np.where(amax > 0, np.frexp(amax)[1] - 1 + 127, 0) - down, 1)
    scale = np.exp2(byte - 127.0)
    codes = (blocks / scale).astype(np.float32).astype(dtype).astype(np.float64)
    return np.moveaxis((codes * scale).reshape(v.shape), -1, axis)


WIDE = False


def mx_kscale(k):
    if not WIDE:
        return np.ones(k)
    levels = np.array([10, -10, 5, -5, 0])
    if k % 512:
        return np.exp2(np.random.permutation(np.resize(levels, k // 32))).repeat(32)
    a = np.empty((k // 512, 16))
    for p in range(k // 512):
        a[p, :8] = np.random.permutation(np.resize(levels, 8))
        for g in range(8):
            far = levels[np.abs(levels - a[p, g]) >= 10]
            a[p, g + 8] = far[np.random.randint(len(far))]
    return np.exp2(a.ravel()).repeat(32)


def f64(x):
    return np.asarray(x).astype(np.float64)


def striped8(idx):
    return np.asarray(idx).reshape(8, -1, 16).transpose(0, 2, 1).reshape(128, -1).astype(np.uint16)


def unstriped8(offs):
    return offs.reshape(8, 16, -1).transpose(0, 2, 1).reshape(8, -1).astype(np.int64)


def pick8(x, idx, run):
    r = np.arange(len(x))
    return x[r[:, None], idx[r % (8 * run) // run]]


E2M1 = np.array([0.0, 0.5, 1.0, 1.5, 2.0, 3.0, 4.0, 6.0, -0.0, -0.5, -1.0, -1.5, -2.0, -3.0, -4.0, -6.0])


def pack_weight(w, fmt):
    k, n = w.shape
    w = f64(np.asarray(w, np.float32).astype(ml_dtypes.bfloat16)).reshape(k // 32, 32, n)
    amax = np.abs(w).max(1)
    if fmt == "e4m3":
        byte = np.frexp(amax)[1] - 1 + 127 - 7
    else:
        mant, ex = np.frexp(amax / 6.0)
        byte = np.where(mant > 0.5, ex, ex - 1) + 127
    byte = np.clip(np.where(amax > 0, byte, 1), 1, 254)
    scaled = (w * np.exp2(127.0 - byte)[:, None, :]).reshape(k, n).astype(np.float32)
    by_word = np.ascontiguousarray(scaled.reshape(k // 512, 128, 4, n).transpose(0, 1, 3, 2))
    if fmt == "e4m3":
        words = by_word.astype(ml_dtypes.float8_e4m3fn).view(np.uint8)
    else:
        c = by_word.astype(ml_dtypes.float4_e2m1fn).view(np.uint8) & 0xF
        words = (c[..., 0::2] | (c[..., 1::2] << 4)).reshape(k // 512, 128, 2 * n)
    return np.ascontiguousarray(words), np.ascontiguousarray(byte.astype(np.uint8).reshape(k // 512, 16, n))


def unpack_weight(words, scales, fmt):
    g, _, n = scales.shape
    words = np.ascontiguousarray(words).reshape(g, 128, n, -1)
    if fmt == "e4m3":
        vals = words.view(ml_dtypes.float8_e4m3fn).astype(np.float64)
    else:
        nib = np.empty((g, 128, n, 4), np.uint8)
        nib[..., 0::2] = words & 0xF
        nib[..., 1::2] = words >> 4
        vals = E2M1[nib]
    vals = vals * np.repeat(np.exp2(scales.astype(np.float64) - 127.0), 8, axis=1)[..., None]
    return vals.transpose(0, 1, 3, 2).reshape(g * 512, n)


D, E, T, Q, I = 512, 512, 1024, 128, 512


def setup_inputs():
    n = np.random.standard_normal
    idx = np.stack([np.random.permutation(T)[:I] for _ in range(8)])
    idx2 = np.stack([np.random.permutation(T)[:I] for _ in range(8)])
    fd = mx_kscale(D)
    fe = mx_kscale(E)
    keysp = pack_weight(n((D, T)) / fd[:, None], "e4m3")
    return {
        "query": (n((D, Q)) * 0.5 / np.sqrt(D) * fd[:, None]).astype(np.float32),
        "keys_words": keysp[0],
        "keys_scales": keysp[1],
        "gout": (n((E, Q)) * 1 / np.sqrt(E) * fe[:, None]).astype(np.float32),
        "vals": (n((E, T)) / fe[:, None]).astype(np.float32),
        "lam": (np.random.uniform(0.3, 1.2, (Q, 1))).astype(np.float32),
        "share": (np.random.uniform(0.3, 1.0, (Q, 1))).astype(np.float32),
        "offs": striped8(idx),
        "offs2": striped8(idx2),
    }


def reference(query, keys_words, keys_scales, gout, vals, lam, share, offs, offs2):
    idx = unstriped8(offs)
    idx2 = unstriped8(offs2)
    keysu = unpack_weight(keys_words, keys_scales, "e4m3")
    queryq = mxq(f64(query), 0, "e4m3")
    a = queryq.T @ keysu
    goutq = mxq(f64(gout), 0, "e4m3")
    valsq = mxq(f64(vals), 0, "e4m3")
    dw = goutq.T @ valsq
    s = pick8(a, idx, 16) + pick8(a, idx2, 16) * f64(lam)
    p = np.exp(s - np.max(s, axis=1, keepdims=True))
    w = p / np.sum(p, axis=1, keepdims=True) * 512.0
    dj = pick8(dw, idx, 16) + pick8(dw, idx2, 16) * f64(share)
    mw = np.sum(w * dj, axis=1, keepdims=True) / 512.0
    ds = w * (dj - mw)
    da = np.zeros((Q, T))
    da[np.arange(Q)[:, None], idx[np.arange(Q) % 128 // 16]] = ds
    db = np.zeros((Q, T))
    db[np.arange(Q)[:, None], idx2[np.arange(Q) % 128 // 16]] = ds
    y = da + db * f64(lam)
    return y

@@ -1,0 +1,184 @@
+from contextlib import ExitStack
+
+import concourse.mybir as mybir
+
+D, E, T, Q, SLOTS = 512, 512, 1024, 128, 512
+FLOPS = 2 * Q * T * (D + E)
+
+F32 = mybir.dt.float32
+BF16 = mybir.dt.bfloat16
+I32 = mybir.dt.int32
+U32 = mybir.dt.uint32
+U16 = mybir.dt.uint16
+U8 = mybir.dt.uint8
+FP8X4 = mybir.dt.float8_e4m3fn_x4
+ALU = mybir.AluOpType
+ACT = mybir.ActivationFunctionType
+
+P = 128
+PACK = 4
+BANK = 512
+HALF = SLOTS // 2
+HALF_COLS = HALF // 16
+VALS_CHUNKS = (256, 256, 256, 128, 128)
+OUT_CHUNK = 256
+
+
+def interleave(copy, grouped, raw):
+    copy(
+        grouped.rearrange("p (c i) j -> p c j i", i=2),
+        raw.rearrange("p j (c i) -> p c j i", i=2),
+    )
+
+
+def tile_attend_gpairs_heads_kernel(tc, query, keys_words, keys_scales, gout, vals, lam, share, offs, offs2, out):
+    nc = tc.nc
+    with ExitStack() as ctx:
+        sb = ctx.enter_context(tc.tile_pool(name="sb", bufs=1))
+        ps = ctx.enter_context(tc.psum_pool(name="ps", bufs=1))
+
+        list1 = sb.tile([P, SLOTS // 16], U16, name="list1")
+        list2 = sb.tile([P, SLOTS // 16], U16, name="list2")
+
+        def load_rows(src, name):
+            raw = sb.tile([P, PACK, src.shape[1]], F32, name=name + "_raw")
+            nc.sync.dma_start(out=raw[:], in_=src.rearrange("(p j) w -> p j w", j=PACK))
+            return raw
+
+        def round_rows(copy, raw, name):
+            grouped = sb.tile([P, raw.shape[2], PACK], BF16, name=name + "_bf", align_bytes=64)
+            interleave(copy, grouped[:], raw[:])
+            return grouped
+
+        def quantize(grouped, name):
+            width = grouped.shape[1]
+            codes = sb.tile([P, width], U32, name=name + "_codes", align_bytes=64)
+            scales = sb.tile([P, width], U8, name=name + "_scales", align_bytes=64)
+            nc.vector.quantize_mx(
+                out=codes[:].bitcast(FP8X4), scales=scales[:], in_=grouped[:].rearrange("p w j -> p (w j)")
+            )
+            return codes, scales
+
+        def product(stationary, codes, scales, name):
+            acc = ps.tile([P, codes.shape[1]], F32, name=name)
+            nc.tensor.matmul_mx(
+                out=acc[:],
+                lhsT=stationary[0][:].bitcast(FP8X4),
+                lhsT_scale=stationary[1][:],
+                rhs=codes.bitcast(FP8X4),
+                rhs_scale=scales,
+                start=True,
+                stop=True,
+            )
+            return acc
+
+        key_scales = sb.tile([P, T], U8, name="key_scales", align_bytes=64)
+        nc.vector.memset(key_scales[:].bitcast(U32), 0)
+        da = sb.tile([P, T], F32, name="da")
+        db = sb.tile([P, T], F32, name="db")
+        nc.vector.memset(da[:], 0.0)
+        nc.vector.memset(db[:], 0.0)
+
+        query_raw = load_rows(query, "query")
+        key_codes = sb.tile([P, T], U32, name="key_codes", align_bytes=64)
+        nc.sync.dma_start(
+            out=key_codes[:].bitcast(I32), in_=keys_words[0].rearrange("p n r -> p (n r)").bitcast(I32)
+        )
+        gout_raw = load_rows(gout, "gout")
+        starts = [sum(VALS_CHUNKS[:c]) for c in range(len(VALS_CHUNKS))]
+        vals_raw = [load_rows(vals[:, starts[0] : starts[0] + VALS_CHUNKS[0]], "vals0")]
+        for quad in range(4):
+            nc.scalar.dma_start(
+                out=key_scales[32 * quad : 32 * quad + 4, :].bitcast(I32),
+                in_=keys_scales[0, 4 * quad : 4 * quad + 4, :].bitcast(I32),
+            )
+        lam_col = sb.tile([P, 1], F32, name="lam_col")
+        share_col = sb.tile([P, 1], F32, name="share_col")
+        nc.gpsimd.dma_start(out=lam_col[:], in_=lam)
+        nc.gpsimd.dma_start(out=share_col[:], in_=share)
+        nc.sync.dma_start(list2[:], offs2)
+        nc.sync.dma_start(list1[:], offs)
+        for c in range(1, len(VALS_CHUNKS)):
+            vals_raw.append(load_rows(vals[:, starts[c] : starts[c] + VALS_CHUNKS[c]], "vals%d" % c))
+
+        warm = sb.tile([P, 1], F32, name="warm")
+        nc.gpsimd.memset(warm[:], 0.0)
+        warm_out = sb.tile([P, 1], F32, name="warm_out")
+        nc.scalar.activation(warm_out[:], warm[:], ACT.Exp)
+
+        query_mx = quantize(round_rows(nc.vector.tensor_copy, query_raw, "query"), "query")
+        lam_row = sb.tile([P, SLOTS], F32, name="lam_row")
+        nc.vector.tensor_copy(lam_row[:], lam_col[:].to_broadcast([P, SLOTS]))
+        share_row = sb.tile([P, SLOTS], F32, name="share_row")
+        nc.vector.tensor_copy(share_row[:], share_col[:].to_broadcast([P, SLOTS]))
+        gout_bf = round_rows(nc.scalar.copy, gout_raw, "gout")
+
+        a = sb.tile([P, T], F32, name="a")
+        for b, copy in enumerate((nc.scalar.copy, nc.vector.tensor_copy)):
+            cols = slice(b * BANK, (b + 1) * BANK)
+            acc = product(query_mx, key_codes[:, cols], key_scales[:, cols], "a_ps%d" % b)
+            copy(a[:, cols], acc[:])
+
+        halves = [(slice(h * HALF, (h + 1) * HALF), slice(h * HALF_COLS, (h + 1) * HALF_COLS)) for h in range(2)]
+
+        def join_pairs(window, factor_row, name):
+            second = sb.tile([P, SLOTS], F32, name=name + "_second")
+            joined = sb.tile([P, SLOTS], F32, name=name)
+            for slots, cols in halves:
+                nc.vector.tensor_tensor(
+                    second[:, slots], window[:].indirect(list2[:, cols]), factor_row[:, slots], ALU.mult
+                )
+            for slots, cols in halves:
+                nc.vector.tensor_tensor(
+                    joined[:, slots], window[:].indirect(list1[:, cols]), second[:, slots], ALU.add
+                )
+            return joined
+
+        gout_mx = quantize(gout_bf, "gout")
+        s = join_pairs(a, lam_row, "s")
+
+        dw = sb.tile([P, T], F32, name="dw")
+        casts = (nc.scalar.copy, nc.scalar.copy, nc.scalar.copy, nc.vector.tensor_copy, nc.vector.tensor_copy)
+        for c, width in enumerate(VALS_CHUNKS):
+            name = "vals%d" % c
+            codes, scales = quantize(round_rows(casts[c], vals_raw[c], name), name)
+            acc = product(gout_mx, codes[:], scales[:], "dw_ps%d" % c)
+            nc.scalar.copy(dw[:, starts[c] : starts[c] + width], acc[:])
+
+        neg_max = sb.tile([P, 1], F32, name="neg_max")
+        nc.vector.tensor_reduce(neg_max[:], s[:], mybir.AxisListType.X, ALU.max, negate=True)
+        p = sb.tile([P, SLOTS], F32, name="p")
+        total = sb.tile([P, 1], F32, name="total")
+        nc.scalar.activation(p[:], s[:], ACT.Exp, bias=neg_max[:], accum_out=total[:])
+        inv_total = sb.tile([P, 1], F32, name="inv_total")
+        nc.vector.reciprocal(inv_total[:], total[:])
+        w_scale = sb.tile([P, 1], F32, name="w_scale")
+        nc.scalar.activation(w_scale[:], inv_total[:], ACT.Copy, scale=512.0)
+        w = sb.tile([P, SLOTS], F32, name="w")
+        nc.scalar.activation(w[:], p[:], ACT.Copy, scale=w_scale[:])
+
+        dj = join_pairs(dw, share_row, "dj")
+        terms = sb.tile([P, SLOTS], F32, name="terms")
+        mean_parts = [sb.tile([P, 1], F32, name="mean_part%d" % h) for h in range(2)]
+        for h, (slots, cols) in enumerate(halves):
+            nc.vector.scalar_tensor_tensor(
+                terms[:, slots], dj[:, slots], inv_total[:], p[:, slots], ALU.mult, ALU.mult,
+                accum_out=mean_parts[h][:],
+            )
+        centred = sb.tile([P, SLOTS], F32, name="centred")
+        for slots, cols in halves:
+            nc.vector.tensor_scalar(
+                centred[:, slots], dj[:, slots], mean_parts[0][:], mean_parts[1][:], ALU.subtract, ALU.subtract
+            )
+        for slots, cols in halves:
+            for window, places in ((da, list1), (db, list2)):
+                nc.vector.tensor_tensor(
+                    window[:].indirect(places[:, cols]), centred[:, slots], w[:, slots], ALU.mult
+                )
+
+        for c in range(T // OUT_CHUNK):
+            cols = slice(c * OUT_CHUNK, (c + 1) * OUT_CHUNK)
+            res = sb.tile([P, OUT_CHUNK], F32, name="res%d" % c)
+            nc.vector.scalar_tensor_tensor(res[:], db[:, cols], lam_col[:], da[:, cols], ALU.mult, ALU.add)
+            queue = nc.sync if c % 2 == 0 else nc.scalar
+            queue.dma_start(out=out[:, cols], in_=res[:])

@@ -41,18 +41,18 @@ def tile_attend_gpairs_heads_kernel(tc, query, keys_words, keys_scales, gout, va
         list2 = sb.tile([P, SLOTS // 16], U16, name="list2")
 
         def load_rows(src, name):
-            raw = sb.tile([P, PACK, src.shape[1]], F32, name=name + "_raw")
+            raw = sb.tile([P, PACK, src.shape[1]], F32, name=name + "_raw", tag=name + "_raw", align_bytes=64)
             nc.sync.dma_start(out=raw[:], in_=src.rearrange("(p j) w -> p j w", j=PACK))
             return raw
 
         def round_rows(copy, raw, name):
-            grouped = sb.tile([P, raw.shape[2], PACK], BF16, name=name + "_bf", align_bytes=64)
+            grouped = sb.tile([P, raw.shape[2], PACK], BF16, name=name + "_bf", tag=name + "_bf", align_bytes=64)
             interleave(copy, grouped[:], raw[:])
             return grouped
 
-        def quantize(grouped, name):
+        def quantize(grouped, name, tag=None):
             width = grouped.shape[1]
-            codes = sb.tile([P, width], U32, name=name + "_codes", align_bytes=64)
+            codes = sb.tile([P, width], U32, name=name + "_codes", tag=tag or name + "_codes", align_bytes=64)
             scales = sb.tile([P, width], U8, name=name + "_scales", align_bytes=64)
             nc.vector.quantize_mx(
                 out=codes[:].bitcast(FP8X4), scales=scales[:], in_=grouped[:].rearrange("p w j -> p (w j)")
@@ -73,57 +73,58 @@ def tile_attend_gpairs_heads_kernel(tc, query, keys_words, keys_scales, gout, va
             return acc
 
         key_scales = sb.tile([P, T], U8, name="key_scales", align_bytes=64)
-        nc.vector.memset(key_scales[:].bitcast(U32), 0)
+        warm = sb.tile([P, 1], F32, name="warm")
+        nc.vector.memset(warm[:], 0.0)
+        warm_out = sb.tile([P, 1], F32, name="warm_out")
+        nc.scalar.activation(warm_out[:], warm[:], ACT.Exp)
+
         da = sb.tile([P, T], F32, name="da")
         db = sb.tile([P, T], F32, name="db")
         nc.vector.memset(da[:], 0.0)
         nc.vector.memset(db[:], 0.0)
 
+        lam_col = sb.tile([P, 1], F32, name="lam_col")
+        share_col = sb.tile([P, 1], F32, name="share_col")
         query_raw = load_rows(query, "query")
-        key_codes = sb.tile([P, T], U32, name="key_codes", align_bytes=64)
-        nc.sync.dma_start(
-            out=key_codes[:].bitcast(I32), in_=keys_words[0].rearrange("p n r -> p (n r)").bitcast(I32)
-        )
-        gout_raw = load_rows(gout, "gout")
-        starts = [sum(VALS_CHUNKS[:c]) for c in range(len(VALS_CHUNKS))]
-        vals_raw = [load_rows(vals[:, starts[0] : starts[0] + VALS_CHUNKS[0]], "vals0")]
         for quad in range(4):
-            nc.scalar.dma_start(
+            nc.sync.dma_start(
                 out=key_scales[32 * quad : 32 * quad + 4, :].bitcast(I32),
                 in_=keys_scales[0, 4 * quad : 4 * quad + 4, :].bitcast(I32),
             )
-        lam_col = sb.tile([P, 1], F32, name="lam_col")
-        share_col = sb.tile([P, 1], F32, name="share_col")
-        nc.gpsimd.dma_start(out=lam_col[:], in_=lam)
-        nc.gpsimd.dma_start(out=share_col[:], in_=share)
+        key_words = keys_words[0].rearrange("p n r -> p (n r)").bitcast(I32)
+        key_codes = []
+        for b in range(T // BANK):
+            codes = sb.tile([P, BANK], U32, name="key_codes%d" % b, align_bytes=64)
+            nc.sync.dma_start(out=codes[:].bitcast(I32), in_=key_words[:, b * BANK : (b + 1) * BANK])
+            key_codes.append(codes)
+        gout_raw = load_rows(gout, "gout")
         nc.sync.dma_start(list2[:], offs2)
+        nc.sync.dma_start(out=lam_col[:], in_=lam)
+        starts = [sum(VALS_CHUNKS[:c]) for c in range(len(VALS_CHUNKS))]
+        vals_raw = [load_rows(vals[:, starts[0] : starts[0] + VALS_CHUNKS[0]], "vals0")]
         nc.sync.dma_start(list1[:], offs)
         for c in range(1, len(VALS_CHUNKS)):
             vals_raw.append(load_rows(vals[:, starts[c] : starts[c] + VALS_CHUNKS[c]], "vals%d" % c))
-
-        warm = sb.tile([P, 1], F32, name="warm")
-        nc.gpsimd.memset(warm[:], 0.0)
-        warm_out = sb.tile([P, 1], F32, name="warm_out")
-        nc.scalar.activation(warm_out[:], warm[:], ACT.Exp)
+            if c == 1:
+                nc.sync.dma_start(out=share_col[:], in_=share)
 
         query_mx = quantize(round_rows(nc.vector.tensor_copy, query_raw, "query"), "query")
-        lam_row = sb.tile([P, SLOTS], F32, name="lam_row")
+        gout_bf = round_rows(nc.vector.tensor_copy, gout_raw, "gout")
+        lam_row = sb.tile([P, SLOTS], F32, name="lam_row", tag="lam_row", align_bytes=64)
         nc.vector.tensor_copy(lam_row[:], lam_col[:].to_broadcast([P, SLOTS]))
-        share_row = sb.tile([P, SLOTS], F32, name="share_row")
-        nc.vector.tensor_copy(share_row[:], share_col[:].to_broadcast([P, SLOTS]))
-        gout_bf = round_rows(nc.scalar.copy, gout_raw, "gout")
+        gout_mx = quantize(gout_bf, "gout")
 
         a = sb.tile([P, T], F32, name="a")
-        for b, copy in enumerate((nc.scalar.copy, nc.vector.tensor_copy)):
+        for b in range(T // BANK):
             cols = slice(b * BANK, (b + 1) * BANK)
-            acc = product(query_mx, key_codes[:, cols], key_scales[:, cols], "a_ps%d" % b)
-            copy(a[:, cols], acc[:])
+            acc = product(query_mx, key_codes[b][:], key_scales[:, cols], "a_ps%d" % b)
+            nc.scalar.copy(a[:, cols], acc[:])
 
         halves = [(slice(h * HALF, (h + 1) * HALF), slice(h * HALF_COLS, (h + 1) * HALF_COLS)) for h in range(2)]
 
-        def join_pairs(window, factor_row, name):
-            second = sb.tile([P, SLOTS], F32, name=name + "_second")
-            joined = sb.tile([P, SLOTS], F32, name=name)
+        def join_pairs(window, factor_row, name, tag):
+            second = sb.tile([P, SLOTS], F32, name=name + "_second", tag=name + "_second", align_bytes=64)
+            joined = sb.tile([P, SLOTS], F32, name=name, tag=tag)
             for slots, cols in halves:
                 nc.vector.tensor_tensor(
                     second[:, slots], window[:].indirect(list2[:, cols]), factor_row[:, slots], ALU.mult
@@ -134,21 +135,24 @@ def tile_attend_gpairs_heads_kernel(tc, query, keys_words, keys_scales, gout, va
                 )
             return joined
 
-        gout_mx = quantize(gout_bf, "gout")
-        s = join_pairs(a, lam_row, "s")
+        s = join_pairs(a, lam_row, "s", "s")
 
-        dw = sb.tile([P, T], F32, name="dw")
         casts = (nc.scalar.copy, nc.scalar.copy, nc.scalar.copy, nc.vector.tensor_copy, nc.vector.tensor_copy)
+        dw_parts = []
         for c, width in enumerate(VALS_CHUNKS):
             name = "vals%d" % c
-            codes, scales = quantize(round_rows(casts[c], vals_raw[c], name), name)
-            acc = product(gout_mx, codes[:], scales[:], "dw_ps%d" % c)
-            nc.scalar.copy(dw[:, starts[c] : starts[c] + width], acc[:])
+            codes, scales = quantize(round_rows(casts[c], vals_raw[c], name), name, "s_second" if c == 0 else None)
+            dw_parts.append(product(gout_mx, codes[:], scales[:], "dw_ps%d" % c))
+        dw = sb.tile([P, T], F32, name="dw", tag="vals2_raw", align_bytes=64)
+        for c, width in enumerate(VALS_CHUNKS):
+            nc.scalar.copy(dw[:, starts[c] : starts[c] + width], dw_parts[c][:])
 
-        neg_max = sb.tile([P, 1], F32, name="neg_max")
+        share_row = sb.tile([P, SLOTS], F32, name="share_row", tag="vals3_bf", align_bytes=64)
+        nc.vector.tensor_copy(share_row[:], share_col[:].to_broadcast([P, SLOTS]))
+        neg_max = sb.tile([P, 1], F32, name="neg_max", tag="vals4_bf", align_bytes=64)
         nc.vector.tensor_reduce(neg_max[:], s[:], mybir.AxisListType.X, ALU.max, negate=True)
         p = sb.tile([P, SLOTS], F32, name="p")
-        total = sb.tile([P, 1], F32, name="total")
+        total = sb.tile([P, 1], F32, name="total", tag="total")
         nc.scalar.activation(p[:], s[:], ACT.Exp, bias=neg_max[:], accum_out=total[:])
         inv_total = sb.tile([P, 1], F32, name="inv_total")
         nc.vector.reciprocal(inv_total[:], total[:])
@@ -157,7 +161,7 @@ def tile_attend_gpairs_heads_kernel(tc, query, keys_words, keys_scales, gout, va
         w = sb.tile([P, SLOTS], F32, name="w")
         nc.scalar.activation(w[:], p[:], ACT.Copy, scale=w_scale[:])
 
-        dj = join_pairs(dw, share_row, "dj")
+        dj = join_pairs(dw, share_row, "dj", "total")
         terms = sb.tile([P, SLOTS], F32, name="terms")
         mean_parts = [sb.tile([P, 1], F32, name="mean_part%d" % h) for h in range(2)]
         for h, (slots, cols) in enumerate(halves):

@@ -21,7 +21,8 @@ BANK = 512
 HALF = SLOTS // 2
 HALF_COLS = HALF // 16
 VALS_CHUNKS = (256, 256, 256, 128, 128)
-OUT_CHUNK = 256
+OUT_CHUNKS = (128, 256, 320, 320)
+A_CHUNK = 256
 
 
 def interleave(copy, grouped, raw):
@@ -59,8 +60,8 @@ def tile_attend_gpairs_heads_kernel(tc, query, keys_words, keys_scales, gout, va
             )
             return codes, scales
 
-        def product(stationary, codes, scales, name):
-            acc = ps.tile([P, codes.shape[1]], F32, name=name)
+        def product(stationary, codes, scales, name, bank):
+            acc = ps.tile([P, codes.shape[1]], F32, name=name, tag="bank%d" % (bank % 8))
             nc.tensor.matmul_mx(
                 out=acc[:],
                 lhsT=stationary[0][:].bitcast(FP8X4),
@@ -110,14 +111,16 @@ def tile_attend_gpairs_heads_kernel(tc, query, keys_words, keys_scales, gout, va
 
         query_mx = quantize(round_rows(nc.vector.tensor_copy, query_raw, "query"), "query")
         gout_bf = round_rows(nc.vector.tensor_copy, gout_raw, "gout")
-        lam_row = sb.tile([P, SLOTS], F32, name="lam_row", tag="lam_row", align_bytes=64)
+        lam_row = sb.tile([P, SLOTS], F32, name="lam_row")
         nc.vector.tensor_copy(lam_row[:], lam_col[:].to_broadcast([P, SLOTS]))
         gout_mx = quantize(gout_bf, "gout")
 
-        a = sb.tile([P, T], F32, name="a")
-        for b in range(T // BANK):
-            cols = slice(b * BANK, (b + 1) * BANK)
-            acc = product(query_mx, key_codes[b][:], key_scales[:, cols], "a_ps%d" % b)
+        a = sb.tile([P, T], F32, name="a", tag="a", align_bytes=64)
+        for b in range(T // A_CHUNK):
+            cols = slice(b * A_CHUNK, (b + 1) * A_CHUNK)
+            first = b * A_CHUNK % BANK
+            codes = key_codes[b * A_CHUNK // BANK][:, first : first + A_CHUNK]
+            acc = product(query_mx, codes, key_scales[:, cols], "a_ps%d" % b, b)
             nc.scalar.copy(a[:, cols], acc[:])
 
         halves = [(slice(h * HALF, (h + 1) * HALF), slice(h * HALF_COLS, (h + 1) * HALF_COLS)) for h in range(2)]
@@ -137,38 +140,45 @@ def tile_attend_gpairs_heads_kernel(tc, query, keys_words, keys_scales, gout, va
 
         s = join_pairs(a, lam_row, "s", "s")
 
-        casts = (nc.scalar.copy, nc.scalar.copy, nc.scalar.copy, nc.vector.tensor_copy, nc.vector.tensor_copy)
+        casts = (nc.scalar.copy, nc.scalar.copy, nc.scalar.copy, nc.scalar.copy, nc.vector.tensor_copy)
         dw_parts = []
         for c, width in enumerate(VALS_CHUNKS):
             name = "vals%d" % c
-            codes, scales = quantize(round_rows(casts[c], vals_raw[c], name), name, "s_second" if c == 0 else None)
-            dw_parts.append(product(gout_mx, codes[:], scales[:], "dw_ps%d" % c))
-        dw = sb.tile([P, T], F32, name="dw", tag="vals2_raw", align_bytes=64)
-        for c, width in enumerate(VALS_CHUNKS):
-            nc.scalar.copy(dw[:, starts[c] : starts[c] + width], dw_parts[c][:])
-
-        share_row = sb.tile([P, SLOTS], F32, name="share_row", tag="vals3_bf", align_bytes=64)
+            codes, scales = quantize(round_rows(casts[c], vals_raw[c], name), name, "a" if c == 0 else None)
+            dw_parts.append(product(gout_mx, codes[:], scales[:], "dw_ps%d" % c, T // A_CHUNK + c))
+        share_row = sb.tile([P, SLOTS], F32, name="share_row", tag="vals3_codes", align_bytes=64)
         nc.vector.tensor_copy(share_row[:], share_col[:].to_broadcast([P, SLOTS]))
         neg_max = sb.tile([P, 1], F32, name="neg_max", tag="vals4_bf", align_bytes=64)
         nc.vector.tensor_reduce(neg_max[:], s[:], mybir.AxisListType.X, ALU.max, negate=True)
+        dw = sb.tile([P, T], F32, name="dw", tag="vals3_raw", align_bytes=64)
+        for c, width in enumerate(VALS_CHUNKS):
+            nc.scalar.copy(dw[:, starts[c] : starts[c] + width], dw_parts[c][:])
+
         p = sb.tile([P, SLOTS], F32, name="p")
         total = sb.tile([P, 1], F32, name="total", tag="total")
         nc.scalar.activation(p[:], s[:], ACT.Exp, bias=neg_max[:], accum_out=total[:])
+
         inv_total = sb.tile([P, 1], F32, name="inv_total")
         nc.vector.reciprocal(inv_total[:], total[:])
         w_scale = sb.tile([P, 1], F32, name="w_scale")
         nc.scalar.activation(w_scale[:], inv_total[:], ACT.Copy, scale=512.0)
-        w = sb.tile([P, SLOTS], F32, name="w")
-        nc.scalar.activation(w[:], p[:], ACT.Copy, scale=w_scale[:])
 
-        dj = join_pairs(dw, share_row, "dj", "total")
+        dj = join_pairs(dw, share_row, "dj", "dj")
         terms = sb.tile([P, SLOTS], F32, name="terms")
+        (slots0, cols0), (slots1, cols1) = halves
+        sum0 = sb.tile([P, 1], F32, name="sum0")
         mean_parts = [sb.tile([P, 1], F32, name="mean_part%d" % h) for h in range(2)]
-        for h, (slots, cols) in enumerate(halves):
-            nc.vector.scalar_tensor_tensor(
-                terms[:, slots], dj[:, slots], inv_total[:], p[:, slots], ALU.mult, ALU.mult,
-                accum_out=mean_parts[h][:],
-            )
+        nc.vector.scalar_tensor_tensor(
+            terms[:, slots0], dj[:, slots0], 1.0, p[:, slots0], ALU.mult, ALU.mult, accum_out=sum0[:]
+        )
+        nc.scalar.activation(mean_parts[0][:], sum0[:], ACT.Copy, scale=inv_total[:])
+        nc.vector.scalar_tensor_tensor(
+            terms[:, slots1], dj[:, slots1], inv_total[:], p[:, slots1], ALU.mult, ALU.mult,
+            accum_out=mean_parts[1][:],
+        )
+        w = sb.tile([P, SLOTS], F32, name="w")
+        for slots, cols in halves:
+            nc.scalar.activation(w[:, slots], p[:, slots], ACT.Copy, scale=w_scale[:])
         centred = sb.tile([P, SLOTS], F32, name="centred")
         for slots, cols in halves:
             nc.vector.tensor_scalar(
@@ -180,9 +190,9 @@ def tile_attend_gpairs_heads_kernel(tc, query, keys_words, keys_scales, gout, va
                     window[:].indirect(places[:, cols]), centred[:, slots], w[:, slots], ALU.mult
                 )
 
-        for c in range(T // OUT_CHUNK):
-            cols = slice(c * OUT_CHUNK, (c + 1) * OUT_CHUNK)
-            res = sb.tile([P, OUT_CHUNK], F32, name="res%d" % c)
+        for c, width in enumerate(OUT_CHUNKS):
+            cols = slice(sum(OUT_CHUNKS[:c]), sum(OUT_CHUNKS[: c + 1]))
+            res = sb.tile([P, width], F32, name="res%d" % c)
             nc.vector.scalar_tensor_tensor(res[:], db[:, cols], lam_col[:], da[:, cols], ALU.mult, ALU.add)
             queue = nc.sync if c % 2 == 0 else nc.scalar
             queue.dma_start(out=out[:, cols], in_=res[:])

@@ -27,8 +27,8 @@ A_CHUNK = 256
 
 def interleave(copy, grouped, raw):
     copy(
-        grouped.rearrange("p (c i) j -> p c j i", i=2),
-        raw.rearrange("p j (c i) -> p c j i", i=2),
+        grouped.rearrange("p (c i) j -> p c j i", i=4),
+        raw.rearrange("p j (c i) -> p c j i", i=4),
     )
 
 
@@ -106,8 +106,7 @@ def tile_attend_gpairs_heads_kernel(tc, query, keys_words, keys_scales, gout, va
         nc.sync.dma_start(list1[:], offs)
         for c in range(1, len(VALS_CHUNKS)):
             vals_raw.append(load_rows(vals[:, starts[c] : starts[c] + VALS_CHUNKS[c]], "vals%d" % c))
-            if c == 1:
-                nc.sync.dma_start(out=share_col[:], in_=share)
+        nc.sync.dma_start(out=share_col[:], in_=share)
 
         query_mx = quantize(round_rows(nc.vector.tensor_copy, query_raw, "query"), "query")
         gout_bf = round_rows(nc.vector.tensor_copy, gout_raw, "gout")

from contextlib import ExitStack

import concourse.mybir as mybir

D, E, T, Q, SLOTS = 512, 512, 1024, 128, 512
FLOPS = 2 * Q * T * (D + E)

F32 = mybir.dt.float32
BF16 = mybir.dt.bfloat16
I32 = mybir.dt.int32
U32 = mybir.dt.uint32
U16 = mybir.dt.uint16
U8 = mybir.dt.uint8
FP8X4 = mybir.dt.float8_e4m3fn_x4
ALU = mybir.AluOpType
ACT = mybir.ActivationFunctionType

P = 128
PACK = 4
BANK = 512
HALF = SLOTS // 2
HALF_COLS = HALF // 16
VALS_CHUNKS = (256, 256, 256, 128, 128)
OUT_CHUNKS = (128, 256, 320, 320)
A_CHUNK = 256


def interleave(copy, grouped, raw):
    copy(
        grouped.rearrange("p (c i) j -> p c j i", i=4),
        raw.rearrange("p j (c i) -> p c j i", i=4),
    )


def tile_attend_gpairs_heads_kernel(tc, query, keys_words, keys_scales, gout, vals, lam, share, offs, offs2, out):
    nc = tc.nc
    with ExitStack() as ctx:
        sb = ctx.enter_context(tc.tile_pool(name="sb", bufs=1))
        ps = ctx.enter_context(tc.psum_pool(name="ps", bufs=1))

        list1 = sb.tile([P, SLOTS // 16], U16, name="list1")
        list2 = sb.tile([P, SLOTS // 16], U16, name="list2")

        def load_rows(src, name):
            raw = sb.tile([P, PACK, src.shape[1]], F32, name=name + "_raw", tag=name + "_raw", align_bytes=64)
            nc.sync.dma_start(out=raw[:], in_=src.rearrange("(p j) w -> p j w", j=PACK))
            return raw

        def round_rows(copy, raw, name):
            grouped = sb.tile([P, raw.shape[2], PACK], BF16, name=name + "_bf", tag=name + "_bf", align_bytes=64)
            interleave(copy, grouped[:], raw[:])
            return grouped

        def quantize(grouped, name, tag=None):
            width = grouped.shape[1]
            codes = sb.tile([P, width], U32, name=name + "_codes", tag=tag or name + "_codes", align_bytes=64)
            scales = sb.tile([P, width], U8, name=name + "_scales", align_bytes=64)
            nc.vector.quantize_mx(
                out=codes[:].bitcast(FP8X4), scales=scales[:], in_=grouped[:].rearrange("p w j -> p (w j)")
            )
            return codes, scales

        def product(stationary, codes, scales, name, bank):
            acc = ps.tile([P, codes.shape[1]], F32, name=name, tag="bank%d" % (bank % 8))
            nc.tensor.matmul_mx(
                out=acc[:],
                lhsT=stationary[0][:].bitcast(FP8X4),
                lhsT_scale=stationary[1][:],
                rhs=codes.bitcast(FP8X4),
                rhs_scale=scales,
                start=True,
                stop=True,
            )
            return acc

        key_scales = sb.tile([P, T], U8, name="key_scales", align_bytes=64)
        warm = sb.tile([P, 1], F32, name="warm")
        nc.vector.memset(warm[:], 0.0)
        warm_out = sb.tile([P, 1], F32, name="warm_out")
        nc.scalar.activation(warm_out[:], warm[:], ACT.Exp)

        da = sb.tile([P, T], F32, name="da")
        db = sb.tile([P, T], F32, name="db")
        nc.vector.memset(da[:], 0.0)
        nc.vector.memset(db[:], 0.0)

        lam_col = sb.tile([P, 1], F32, name="lam_col")
        share_col = sb.tile([P, 1], F32, name="share_col")
        query_raw = load_rows(query, "query")
        for quad in range(4):
            nc.sync.dma_start(
                out=key_scales[32 * quad : 32 * quad + 4, :].bitcast(I32),
                in_=keys_scales[0, 4 * quad : 4 * quad + 4, :].bitcast(I32),
            )
        key_words = keys_words[0].rearrange("p n r -> p (n r)").bitcast(I32)
        key_codes = []
        for b in range(T // BANK):
            codes = sb.tile([P, BANK], U32, name="key_codes%d" % b, align_bytes=64)
            nc.sync.dma_start(out=codes[:].bitcast(I32), in_=key_words[:, b * BANK : (b + 1) * BANK])
            key_codes.append(codes)
        gout_raw = load_rows(gout, "gout")
        nc.sync.dma_start(list2[:], offs2)
        nc.sync.dma_start(out=lam_col[:], in_=lam)
        starts = [sum(VALS_CHUNKS[:c]) for c in range(len(VALS_CHUNKS))]
        vals_raw = [load_rows(vals[:, starts[0] : starts[0] + VALS_CHUNKS[0]], "vals0")]
        nc.sync.dma_start(list1[:], offs)
        for c in range(1, len(VALS_CHUNKS)):
            vals_raw.append(load_rows(vals[:, starts[c] : starts[c] + VALS_CHUNKS[c]], "vals%d" % c))
        nc.sync.dma_start(out=share_col[:], in_=share)

        query_mx = quantize(round_rows(nc.vector.tensor_copy, query_raw, "query"), "query")
        gout_bf = round_rows(nc.vector.tensor_copy, gout_raw, "gout")
        lam_row = sb.tile([P, SLOTS], F32, name="lam_row")
        nc.vector.tensor_copy(lam_row[:], lam_col[:].to_broadcast([P, SLOTS]))
        gout_mx = quantize(gout_bf, "gout")

        a = sb.tile([P, T], F32, name="a", tag="a", align_bytes=64)
        for b in range(T // A_CHUNK):
            cols = slice(b * A_CHUNK, (b + 1) * A_CHUNK)
            first = b * A_CHUNK % BANK
            codes = key_codes[b * A_CHUNK // BANK][:, first : first + A_CHUNK]
            acc = product(query_mx, codes, key_scales[:, cols], "a_ps%d" % b, b)
            nc.scalar.copy(a[:, cols], acc[:])

        halves = [(slice(h * HALF, (h + 1) * HALF), slice(h * HALF_COLS, (h + 1) * HALF_COLS)) for h in range(2)]

        def join_pairs(window, factor_row, name, tag):
            second = sb.tile([P, SLOTS], F32, name=name + "_second", tag=name + "_second", align_bytes=64)
            joined = sb.tile([P, SLOTS], F32, name=name, tag=tag)
            for slots, cols in halves:
                nc.vector.tensor_tensor(
                    second[:, slots], window[:].indirect(list2[:, cols]), factor_row[:, slots], ALU.mult
                )
            for slots, cols in halves:
                nc.vector.tensor_tensor(
                    joined[:, slots], window[:].indirect(list1[:, cols]), second[:, slots], ALU.add
                )
            return joined

        s = join_pairs(a, lam_row, "s", "s")

        casts = (nc.scalar.copy, nc.scalar.copy, nc.scalar.copy, nc.scalar.copy, nc.vector.tensor_copy)
        dw_parts = []
        for c, width in enumerate(VALS_CHUNKS):
            name = "vals%d" % c
            codes, scales = quantize(round_rows(casts[c], vals_raw[c], name), name, "a" if c == 0 else None)
            dw_parts.append(product(gout_mx, codes[:], scales[:], "dw_ps%d" % c, T // A_CHUNK + c))
        share_row = sb.tile([P, SLOTS], F32, name="share_row", tag="vals3_codes", align_bytes=64)
        nc.vector.tensor_copy(share_row[:], share_col[:].to_broadcast([P, SLOTS]))
        neg_max = sb.tile([P, 1], F32, name="neg_max", tag="vals4_bf", align_bytes=64)
        nc.vector.tensor_reduce(neg_max[:], s[:], mybir.AxisListType.X, ALU.max, negate=True)
        dw = sb.tile([P, T], F32, name="dw", tag="vals3_raw", align_bytes=64)
        for c, width in enumerate(VALS_CHUNKS):
            nc.scalar.copy(dw[:, starts[c] : starts[c] + width], dw_parts[c][:])

        p = sb.tile([P, SLOTS], F32, name="p")
        total = sb.tile([P, 1], F32, name="total", tag="total")
        nc.scalar.activation(p[:], s[:], ACT.Exp, bias=neg_max[:], accum_out=total[:])

        inv_total = sb.tile([P, 1], F32, name="inv_total")
        nc.vector.reciprocal(inv_total[:], total[:])
        w_scale = sb.tile([P, 1], F32, name="w_scale")
        nc.scalar.activation(w_scale[:], inv_total[:], ACT.Copy, scale=512.0)

        dj = join_pairs(dw, share_row, "dj", "dj")
        terms = sb.tile([P, SLOTS], F32, name="terms")
        (slots0, cols0), (slots1, cols1) = halves
        sum0 = sb.tile([P, 1], F32, name="sum0")
        mean_parts = [sb.tile([P, 1], F32, name="mean_part%d" % h) for h in range(2)]
        nc.vector.scalar_tensor_tensor(
            terms[:, slots0], dj[:, slots0], 1.0, p[:, slots0], ALU.mult, ALU.mult, accum_out=sum0[:]
        )
        nc.scalar.activation(mean_parts[0][:], sum0[:], ACT.Copy, scale=inv_total[:])
        nc.vector.scalar_tensor_tensor(
            terms[:, slots1], dj[:, slots1], inv_total[:], p[:, slots1], ALU.mult, ALU.mult,
            accum_out=mean_parts[1][:],
        )
        w = sb.tile([P, SLOTS], F32, name="w")
        for slots, cols in halves:
            nc.scalar.activation(w[:, slots], p[:, slots], ACT.Copy, scale=w_scale[:])
        centred = sb.tile([P, SLOTS], F32, name="centred")
        for slots, cols in halves:
            nc.vector.tensor_scalar(
                centred[:, slots], dj[:, slots], mean_parts[0][:], mean_parts[1][:], ALU.subtract, ALU.subtract
            )
        for slots, cols in halves:
            for window, places in ((da, list1), (db, list2)):
                nc.vector.tensor_tensor(
                    window[:].indirect(places[:, cols]), centred[:, slots], w[:, slots], ALU.mult
                )

        for c, width in enumerate(OUT_CHUNKS):
            cols = slice(sum(OUT_CHUNKS[:c]), sum(OUT_CHUNKS[: c + 1]))
            res = sb.tile([P, width], F32, name="res%d" % c)
            nc.vector.scalar_tensor_tensor(res[:], db[:, cols], lam_col[:], da[:, cols], ALU.mult, ALU.add)
            queue = nc.sync if c % 2 == 0 else nc.scalar
            queue.dma_start(out=out[:, cols], in_=res[:])
